import numpy as np
import ml_dtypes


def mxq(x, axis, fmt="e4m3"):
    dtype, down = {"e4m3": (ml_dtypes.float8_e4m3fn, 7), "e5m2": (ml_dtypes.float8_e5m2, 14)}[fmt]
    v = np.moveaxis(np.asarray(x, np.float32).astype(ml_dtypes.bfloat16).astype(np.float64), axis, -1)
    blocks = v.reshape(v.shape[:-1] + (-1, 32))
    amax = np.abs(blocks).max(-1, keepdims=True)
    byte = np.maximum(np.where(amax > 0, np.frexp(amax)[1] - 1 + 127, 0) - down, 1)
    scale = np.exp2(byte - 127.0)
    codes = (blocks / scale).astype(np.float32).astype(dtype).astype(np.float64)
    return np.moveaxis((codes * scale).reshape(v.shape), -1, axis)


WIDE = False


def mx_kscale(k):
    if not WIDE:
        return np.ones(k)
    levels = np.array([10, -10, 5, -5, 0])
    if k % 512:
        return np.exp2(np.random.permutation(np.resize(levels, k // 32))).repeat(32)
    a = np.empty((k // 512, 16))
    for p in range(k // 512):
        a[p, :8] = np.random.permutation(np.resize(levels, 8))
        for g in range(8):
            far = levels[np.abs(levels - a[p, g]) >= 10]
            a[p, g + 8] = far[np.random.randint(len(far))]
    return np.exp2(a.ravel()).repeat(32)


def f64(x):
    return np.asarray(x).astype(np.float64)


def striped(idx):
    return np.tile(idx.reshape(-1, 16).T, (8, 1)).astype(np.uint16)


def unstriped(offs):
    return offs[:16].T.reshape(-1).astype(np.int64)


def pack_weight(w):
    k, n = w.shape
    w = f64(np.asarray(w, np.float32).astype(ml_dtypes.bfloat16)).reshape(k // 32, 32, n)
    amax = np.abs(w).max(1)
    byte = np.clip(np.where(amax > 0, np.frexp(amax)[1] - 1 + 127 - 7, 1), 1, 254)
    scaled = (w * np.exp2(127.0 - byte)[:, None, :]).reshape(k, n).astype(np.float32)
    words = np.ascontiguousarray(scaled.reshape(k // 512, 128, 4, n).transpose(0, 1, 3, 2)).astype(ml_dtypes.float8_e4m3fn).view(np.uint8)
    return words, np.ascontiguousarray(byte.astype(np.uint8).reshape(k // 512, 16, n))


def unpack_weight(words, scales):
    g, p, n, _ = words.shape
    vals = np.ascontiguousarray(words).view(ml_dtypes.float8_e4m3fn).astype(np.float64) * np.repeat(np.exp2(scales.astype(np.float64) - 127.0), 8, axis=1)[..., None]
    return vals.transpose(0, 1, 3, 2).reshape(g * 512, n)


def relu(v):
    return np.maximum(v, 0.0)


K, T, N = 512, 512, 128


def setup_inputs():
    n = np.random.standard_normal
    s = mx_kscale(K)[:, None]
    packed_xT = pack_weight(n((K, T)) * s)
    return {
        "x_words": packed_xT[0],
        "x_scales": packed_xT[1],
        "w1": (n((K, N)) / np.sqrt(K) / s).astype(np.float32),
        "w2": (n((K, N)) / np.sqrt(K) / s).astype(np.float32),
        "w3": (n((K, N)) / np.sqrt(K) / s).astype(np.float32),
        "pos1": striped(np.random.permutation(T)),
        "pos2": striped(np.random.permutation(T)),
        "pos3": striped(np.random.permutation(T)),
    }


def reference(x_words, x_scales, w1, w2, w3, pos1, pos2, pos3):
    xq = unpack_weight(x_words, x_scales)
    h = mxq(f64(w3), 0, "e4m3").T @ xq
    g = mxq(f64(w1), 0, "e4m3").T @ xq
    s = mxq(f64(w2), 0, "e4m3").T @ xq
    return relu(h[:, unstriped(pos1)] * g + s) + relu(h[:, unstriped(pos2)] * g + s) + relu(h[:, unstriped(pos3)] * g + s)

@@ -1,0 +1,138 @@
+from contextlib import ExitStack
+
+import concourse.mybir as mybir
+from concourse.masks import make_identity
+
+K, T, N = 512, 512, 128
+FLOPS = 3 * 2 * K * T * N
+
+F32 = mybir.dt.float32
+BF16 = mybir.dt.bfloat16
+I32 = mybir.dt.int32
+U32 = mybir.dt.uint32
+U16 = mybir.dt.uint16
+U8 = mybir.dt.uint8
+FP8X4 = mybir.dt.float8_e4m3fn_x4
+ALU = mybir.AluOpType
+ACT = mybir.ActivationFunctionType
+
+P = 128
+PACK = 4
+HALF = T // 2
+
+
+def tile_picked_wfilmg_relu_l_kernel(tc, x_words, x_scales, w1, w2, w3, pos1, pos2, pos3, out):
+    nc = tc.nc
+    with ExitStack() as ctx:
+        sb = ctx.enter_context(tc.tile_pool(name="sb", bufs=1))
+        ps = ctx.enter_context(tc.psum_pool(name="ps", bufs=1))
+
+        def bank(b, width, name):
+            return ps.tile([P, width], F32, name=name, tag="bank%d" % b)
+
+        cols = [slice(0, HALF), slice(HALF, T)]
+        offs = [slice(0, HALF // 16), slice(HALF // 16, T // 16)]
+
+        xs = sb.tile([P, T], U8, name="xs", align_bytes=64)
+        nc.gpsimd.memset(xs[:].bitcast(U32), 0)
+
+        raw = {}
+        for name, w in (("w3", w3), ("w1", w1)):
+            raw[name] = sb.tile([P, PACK, N], F32, name="raw_" + name)
+            nc.sync.dma_start(out=raw[name][:], in_=w.rearrange("(p j) m -> p j m", j=PACK))
+        for q in range(4):
+            nc.scalar.dma_start(out=xs[32 * q : 32 * q + 4, :].bitcast(I32), in_=x_scales[0, 4 * q : 4 * q + 4, :].bitcast(I32))
+        x_flat = x_words[0].rearrange("p n t -> p (n t)")
+        xw = sb.tile([P, T], U32, name="xw", align_bytes=64)
+        nc.sync.dma_start(out=xw[:].bitcast(I32), in_=x_flat.bitcast(I32))
+        raw["w2"] = sb.tile([P, PACK, N], F32, name="raw_w2")
+        nc.sync.dma_start(out=raw["w2"][:], in_=w2.rearrange("(p j) m -> p j m", j=PACK))
+        lists = [sb.tile([P, T // 16], U16, name="pos%d" % d) for d in range(3)]
+        nc.sync.dma_start(lists[0][:], pos1)
+        nc.sync.dma_start(lists[1][:], pos2)
+        nc.sync.dma_start(lists[2][:], pos3)
+
+        ident = sb.tile([P, P], F32, name="ident")
+        make_identity(nc, ident[:])
+
+        grouped, codes, scales = {}, {}, {}
+        for name in ("w3", "w1", "w2"):
+            grouped[name] = sb.tile([P, N, PACK], BF16, name="grouped_" + name, align_bytes=64)
+            codes[name] = sb.tile([P, N], U32, name="codes_" + name, align_bytes=64)
+            scales[name] = sb.tile([P, N], U8, name="scales_" + name, align_bytes=64)
+
+        def quantize(name):
+            nc.vector.quantize_mx(out=codes[name][:].bitcast(FP8X4), scales=scales[name][:], in_=grouped[name][:].rearrange("p m j -> p (m j)"))
+
+        def product(dst, name, c):
+            nc.tensor.matmul_mx(out=dst, lhsT=codes[name][:].bitcast(FP8X4), lhsT_scale=scales[name][:], rhs=xw[:, cols[c]].bitcast(FP8X4), rhs_scale=xs[:, cols[c]], start=True, stop=True)
+
+        nc.vector.tensor_copy(out=grouped["w3"][:], in_=raw["w3"][:].rearrange("p j m -> p m j"))
+        quantize("w3")
+        nc.scalar.copy(out=grouped["w1"][:], in_=raw["w1"][:].rearrange("p j m -> p m j"))
+        quantize("w1")
+
+        h = sb.tile([P, T], F32, name="h")
+        g = sb.tile([P, T], F32, name="g")
+        s = sb.tile([P, T], F32, name="s")
+        h_ps = [bank(c, HALF, "h_ps%d" % c) for c in range(2)]
+        g_ps = [bank(2 + c, HALF, "g_ps%d" % c) for c in range(2)]
+        for c in range(2):
+            product(h_ps[c][:], "w3", c)
+        for c in range(2):
+            product(g_ps[c][:], "w1", c)
+        nc.scalar.copy(out=h[:, cols[0]], in_=h_ps[0][:])
+        nc.vector.tensor_copy(out=grouped["w2"][:], in_=raw["w2"][:].rearrange("p j m -> p m j"))
+        nc.vector.tensor_copy(out=h[:, cols[1]], in_=h_ps[1][:])
+        quantize("w2")
+        nc.scalar.copy(out=g[:, cols[0]], in_=g_ps[0][:])
+        nc.scalar.copy(out=g[:, cols[1]], in_=g_ps[1][:])
+
+        scaled = [[sb.tile([P, HALF], F32, name="scaled%d_%d" % (d, c)) for c in range(2)] for d in range(3)]
+
+        def gather(d, c):
+            nc.vector.tensor_tensor(scaled[d][c][:], h[:].indirect(lists[d][:, offs[c]]), g[:, cols[c]], ALU.mult)
+
+        s_ps = [bank(4 + c, HALF, "s_ps%d" % c) for c in range(2)]
+        for c in range(2):
+            product(s_ps[c][:], "w2", c)
+            nc.scalar.copy(out=s[:, cols[c]], in_=s_ps[c][:])
+        gather(0, 0)
+        gather(0, 1)
+
+        def turn(dst, src, start, stop):
+            for b in range(2):
+                blk = slice(b * P, (b + 1) * P)
+                nc.tensor.matmul(dst[:, blk], src[:, blk], ident[:], start=(start and b == 0), stop=(stop and b == 1), is_transpose=True)
+
+        u_bank = {(0, 0): 6, (0, 1): 7, (1, 0): 0, (1, 1): 1}
+        relu_t = {}
+
+        def film(d, c):
+            u = bank(u_bank[(d, c)], HALF, "u%d_%d" % (d, c))
+            first, second = (scaled[d][c][:], s[:, cols[c]]) if (d, c) == (0, 0) else (s[:, cols[c]], scaled[d][c][:])
+            turn(u, first, True, False)
+            turn(u, second, False, True)
+            relu_t[(d, c)] = sb.tile([P, HALF], F32, name="relu%d_%d" % (d, c))
+            nc.scalar.activation(relu_t[(d, c)][:], u[:], ACT.Relu)
+
+        film(0, 0)
+        film(0, 1)
+        gather(1, 0)
+        gather(1, 1)
+        acc = [bank(2 + c, HALF, "acc%d" % c) for c in range(2)]
+        film(1, 0)
+        turn(acc[0], relu_t[(0, 0)], True, False)
+        turn(acc[1], relu_t[(0, 1)], True, False)
+        film(1, 1)
+        turn(acc[0], relu_t[(1, 0)], False, True)
+        turn(acc[1], relu_t[(1, 1)], False, True)
+        gather(2, 0)
+        gather(2, 1)
+        last = [sb.tile([P, HALF], F32, name="last%d" % c) for c in range(2)]
+        res = [sb.tile([P, HALF], F32, name="res%d" % c) for c in range(2)]
+        for c in range(2):
+            nc.vector.tensor_tensor(last[c][:], scaled[2][c][:], s[:, cols[c]], ALU.add)
+        for c in range(2):
+            nc.vector.scalar_tensor_tensor(res[c][:], last[c][:], 0.0, acc[c][:], ALU.max, ALU.add)
+            (nc.sync if c == 0 else nc.scalar).dma_start(out=out[:, cols[c]], in_=res[c][:])

@@ -18,7 +18,16 @@ ACT = mybir.ActivationFunctionType
 
 P = 128
 PACK = 4
-HALF = T // 2
+QUADRANT = 32
+LIST_COLS = P // 16
+
+HALVES = ((0, 2), (2, 4))
+SMALL_FIRST = ((0, 1), (1, 2), (2, 4))
+SMALL_LAST = ((0, 2), (2, 3), (3, 4))
+
+
+def columns(lo, hi):
+    return slice(lo * P, hi * P)
 
 
 def tile_picked_wfilmg_relu_l_kernel(tc, x_words, x_scales, w1, w2, w3, pos1, pos2, pos3, out):
@@ -27,112 +36,143 @@ def tile_picked_wfilmg_relu_l_kernel(tc, x_words, x_scales, w1, w2, w3, pos1, po
         sb = ctx.enter_context(tc.tile_pool(name="sb", bufs=1))
         ps = ctx.enter_context(tc.psum_pool(name="ps", bufs=1))
 
-        def bank(b, width, name):
-            return ps.tile([P, width], F32, name=name, tag="bank%d" % b)
+        def bank(number, strips, name):
+            return ps.tile([P, strips * P], F32, name=name, tag="bank%d" % number)
 
-        cols = [slice(0, HALF), slice(HALF, T)]
-        offs = [slice(0, HALF // 16), slice(HALF // 16, T // 16)]
+        x_plane = sb.tile([P, T], U8, name="x_plane", align_bytes=64)
+        nc.gpsimd.memset(x_plane[:].bitcast(U32), 0)
 
-        xs = sb.tile([P, T], U8, name="xs", align_bytes=64)
-        nc.gpsimd.memset(xs[:].bitcast(U32), 0)
+        staged = {}
 
-        raw = {}
-        for name, w in (("w3", w3), ("w1", w1)):
-            raw[name] = sb.tile([P, PACK, N], F32, name="raw_" + name)
-            nc.sync.dma_start(out=raw[name][:], in_=w.rearrange("(p j) m -> p j m", j=PACK))
-        for q in range(4):
-            nc.scalar.dma_start(out=xs[32 * q : 32 * q + 4, :].bitcast(I32), in_=x_scales[0, 4 * q : 4 * q + 4, :].bitcast(I32))
-        x_flat = x_words[0].rearrange("p n t -> p (n t)")
-        xw = sb.tile([P, T], U32, name="xw", align_bytes=64)
-        nc.sync.dma_start(out=xw[:].bitcast(I32), in_=x_flat.bitcast(I32))
-        raw["w2"] = sb.tile([P, PACK, N], F32, name="raw_w2")
-        nc.sync.dma_start(out=raw["w2"][:], in_=w2.rearrange("(p j) m -> p j m", j=PACK))
-        lists = [sb.tile([P, T // 16], U16, name="pos%d" % d) for d in range(3)]
-        nc.sync.dma_start(lists[0][:], pos1)
-        nc.sync.dma_start(lists[1][:], pos2)
-        nc.sync.dma_start(lists[2][:], pos3)
+        def load_weight(name, w):
+            staged[name] = sb.tile([P, PACK, N], F32, name="staged_" + name)
+            nc.sync.dma_start(out=staged[name][:], in_=w.rearrange("(p t) m -> p t m", t=PACK))
 
-        ident = sb.tile([P, P], F32, name="ident")
-        make_identity(nc, ident[:])
+        load_weight("w3", w3)
+        load_weight("w1", w1)
+        for q in range(P // QUADRANT):
+            nc.sync.dma_start(
+                out=x_plane[QUADRANT * q : QUADRANT * q + 4, :].bitcast(I32),
+                in_=x_scales[0, 4 * q : 4 * q + 4, :].bitcast(I32),
+            )
+        x_codes = sb.tile([P, T], U32, name="x_codes", align_bytes=64)
+        nc.sync.dma_start(out=x_codes[:].bitcast(I32), in_=x_words[0].rearrange("p n t -> p (n t)").bitcast(I32))
+        load_weight("w2", w2)
+        lists = [sb.tile([P, T // 16], U16, name="list%d" % d) for d in range(3)]
+        for offsets, pos in zip(lists, (pos1, pos2, pos3)):
+            nc.sync.dma_start(offsets[:], pos)
 
-        grouped, codes, scales = {}, {}, {}
+        identity = sb.tile([P, P], F32, name="identity")
+        make_identity(nc, identity[:])
+
+        grouped, codes, planes = {}, {}, {}
         for name in ("w3", "w1", "w2"):
-            grouped[name] = sb.tile([P, N, PACK], BF16, name="grouped_" + name, align_bytes=64)
+            grouped[name] = sb.tile([P, N, PACK], BF16, name="grouped_" + name, tag="grouped_" + name, align_bytes=64)
             codes[name] = sb.tile([P, N], U32, name="codes_" + name, align_bytes=64)
-            scales[name] = sb.tile([P, N], U8, name="scales_" + name, align_bytes=64)
+            planes[name] = sb.tile([P, N], U8, name="plane_" + name, align_bytes=64)
 
-        def quantize(name):
-            nc.vector.quantize_mx(out=codes[name][:].bitcast(FP8X4), scales=scales[name][:], in_=grouped[name][:].rearrange("p m j -> p (m j)"))
+        def quantise(name):
+            nc.vector.tensor_copy(out=grouped[name][:], in_=staged[name][:].rearrange("p t m -> p m t"))
+            nc.vector.quantize_mx(
+                out=codes[name][:].bitcast(FP8X4),
+                scales=planes[name][:],
+                in_=grouped[name][:].rearrange("p m t -> p (m t)"),
+            )
 
-        def product(dst, name, c):
-            nc.tensor.matmul_mx(out=dst, lhsT=codes[name][:].bitcast(FP8X4), lhsT_scale=scales[name][:], rhs=xw[:, cols[c]].bitcast(FP8X4), rhs_scale=xs[:, cols[c]], start=True, stop=True)
+        def project(name, lo, hi, number):
+            sums = bank(number, hi - lo, "%s_x%d" % (name, lo))
+            nc.tensor.matmul_mx(
+                out=sums[:],
+                lhsT=codes[name][:].bitcast(FP8X4),
+                lhsT_scale=planes[name][:],
+                rhs=x_codes[:, columns(lo, hi)].bitcast(FP8X4),
+                rhs_scale=x_plane[:, columns(lo, hi)],
+                start=True,
+                stop=True,
+            )
+            return sums
 
-        nc.vector.tensor_copy(out=grouped["w3"][:], in_=raw["w3"][:].rearrange("p j m -> p m j"))
-        quantize("w3")
-        nc.scalar.copy(out=grouped["w1"][:], in_=raw["w1"][:].rearrange("p j m -> p m j"))
-        quantize("w1")
-
+        quantise("w3")
+        quantise("w1")
         h = sb.tile([P, T], F32, name="h")
         g = sb.tile([P, T], F32, name="g")
         s = sb.tile([P, T], F32, name="s")
-        h_ps = [bank(c, HALF, "h_ps%d" % c) for c in range(2)]
-        g_ps = [bank(2 + c, HALF, "g_ps%d" % c) for c in range(2)]
-        for c in range(2):
-            product(h_ps[c][:], "w3", c)
-        for c in range(2):
-            product(g_ps[c][:], "w1", c)
-        nc.scalar.copy(out=h[:, cols[0]], in_=h_ps[0][:])
-        nc.vector.tensor_copy(out=grouped["w2"][:], in_=raw["w2"][:].rearrange("p j m -> p m j"))
-        nc.vector.tensor_copy(out=h[:, cols[1]], in_=h_ps[1][:])
-        quantize("w2")
-        nc.scalar.copy(out=g[:, cols[0]], in_=g_ps[0][:])
-        nc.scalar.copy(out=g[:, cols[1]], in_=g_ps[1][:])
+        h_sums = [project("w3", lo, hi, i) for i, (lo, hi) in enumerate(HALVES)]
+        g_sums = [project("w1", lo, hi, 2 + i) for i, (lo, hi) in enumerate(SMALL_FIRST)]
+        for (lo, hi), sums in zip(HALVES, h_sums):
+            nc.scalar.copy(out=h[:, columns(lo, hi)], in_=sums[:])
+        quantise("w2")
+        for (lo, hi), sums in zip(SMALL_FIRST, g_sums):
+            nc.scalar.copy(out=g[:, columns(lo, hi)], in_=sums[:])
+        for i, (lo, hi) in enumerate(SMALL_FIRST):
+            nc.scalar.copy(out=s[:, columns(lo, hi)], in_=project("w2", lo, hi, 5 + i)[:])
 
-        scaled = [[sb.tile([P, HALF], F32, name="scaled%d_%d" % (d, c)) for c in range(2)] for d in range(3)]
+        scaled = {}
 
-        def gather(d, c):
-            nc.vector.tensor_tensor(scaled[d][c][:], h[:].indirect(lists[d][:, offs[c]]), g[:, cols[c]], ALU.mult)
+        def gather(d, lo, hi, tag=None):
+            name = "scaled%d_%d" % (d, lo)
+            piece = sb.tile([P, (hi - lo) * P], F32, name=name, tag=tag or name, align_bytes=64)
+            window = h[:].indirect(lists[d][:, lo * LIST_COLS : hi * LIST_COLS])
+            nc.vector.tensor_tensor(piece[:], window, g[:, columns(lo, hi)], ALU.mult)
+            for strip in range(lo, hi):
+                scaled[d, strip] = piece[:, columns(strip - lo, strip - lo + 1)]
+            return piece
 
-        s_ps = [bank(4 + c, HALF, "s_ps%d" % c) for c in range(2)]
-        for c in range(2):
-            product(s_ps[c][:], "w2", c)
-            nc.scalar.copy(out=s[:, cols[c]], in_=s_ps[c][:])
-        gather(0, 0)
-        gather(0, 1)
+        gather(0, *SMALL_FIRST[0])
+        gather(0, *SMALL_FIRST[1], tag="grouped_w2")
+        gather(0, *SMALL_FIRST[2])
+        for lo, hi in SMALL_LAST:
+            gather(1, lo, hi)
 
-        def turn(dst, src, start, stop):
-            for b in range(2):
-                blk = slice(b * P, (b + 1) * P)
-                nc.tensor.matmul(dst[:, blk], src[:, blk], ident[:], start=(start and b == 0), stop=(stop and b == 1), is_transpose=True)
+        film = {}
+        for number, (d, lo, hi) in enumerate(((0, 0, 2), (0, 2, 4), (1, 0, 2), (1, 2, 3), (1, 3, 4))):
+            film[d, lo] = bank(number, hi - lo, "film%d_%d" % (d, lo))
+        totals = {lo: bank(5 + i, hi - lo, "total%d" % lo) for i, (lo, hi) in enumerate(HALVES)}
+        rectified = [sb.tile([P, T], F32, name="rectified%d" % d) for d in range(2)]
 
-        u_bank = {(0, 0): 6, (0, 1): 7, (1, 0): 0, (1, 1): 1}
-        relu_t = {}
+        def turn(target, slot, source, start, stop):
+            nc.tensor.matmul(
+                target[:, columns(slot, slot + 1)], source, identity[:], start=start, stop=stop, is_transpose=True
+            )
 
-        def film(d, c):
-            u = bank(u_bank[(d, c)], HALF, "u%d_%d" % (d, c))
-            first, second = (scaled[d][c][:], s[:, cols[c]]) if (d, c) == (0, 0) else (s[:, cols[c]], scaled[d][c][:])
-            turn(u, first, True, False)
-            turn(u, second, False, True)
-            relu_t[(d, c)] = sb.tile([P, HALF], F32, name="relu%d_%d" % (d, c))
-            nc.scalar.activation(relu_t[(d, c)][:], u[:], ACT.Relu)
+        def turn_s(d, lo, hi):
+            for strip in range(lo, hi):
+                turn(film[d, lo], strip - lo, s[:, columns(strip, strip + 1)], strip == lo, False)
 
-        film(0, 0)
-        film(0, 1)
-        gather(1, 0)
-        gather(1, 1)
-        acc = [bank(2 + c, HALF, "acc%d" % c) for c in range(2)]
-        film(1, 0)
-        turn(acc[0], relu_t[(0, 0)], True, False)
-        turn(acc[1], relu_t[(0, 1)], True, False)
-        film(1, 1)
-        turn(acc[0], relu_t[(1, 0)], False, True)
-        turn(acc[1], relu_t[(1, 1)], False, True)
-        gather(2, 0)
-        gather(2, 1)
-        last = [sb.tile([P, HALF], F32, name="last%d" % c) for c in range(2)]
-        res = [sb.tile([P, HALF], F32, name="res%d" % c) for c in range(2)]
-        for c in range(2):
-            nc.vector.tensor_tensor(last[c][:], scaled[2][c][:], s[:, cols[c]], ALU.add)
-        for c in range(2):
-            nc.vector.scalar_tensor_tensor(res[c][:], last[c][:], 0.0, acc[c][:], ALU.max, ALU.add)
-            (nc.sync if c == 0 else nc.scalar).dma_start(out=out[:, cols[c]], in_=res[c][:])
+        def rectify(d, lo, hi):
+            nc.scalar.activation(rectified[d][:, columns(lo, hi)], film[d, lo][:], ACT.Relu)
+
+        def turn_scaled(d, lo, hi):
+            for strip in range(lo, hi):
+                turn(film[d, lo], strip - lo, scaled[d, strip], False, strip == hi - 1)
+            rectify(d, lo, hi)
+
+        def turn_back(d, lo, hi):
+            for strip in range(lo, hi):
+                first, last = d == 0 and strip == lo, d == 1 and strip == hi - 1
+                turn(totals[lo], strip - lo, rectified[d][:, columns(strip, strip + 1)], first, last)
+
+        for strip in range(2):
+            turn(film[0, 0], strip, scaled[0, strip], strip == 0, False)
+            turn(film[0, 0], strip, s[:, columns(strip, strip + 1)], False, strip == 1)
+        rectify(0, 0, 2)
+        turn_s(1, 0, 2)
+        turn_s(0, 2, 4)
+        turn_scaled(0, 2, 4)
+        turn_scaled(1, 0, 2)
+        turn_back(0, 0, 2)
+        for lo, hi in SMALL_LAST[1:]:
+            turn_s(1, lo, hi)
+            turn_scaled(1, lo, hi)
+        turn_back(0, 2, 4)
+        for lo, hi in HALVES:
+            turn_back(1, lo, hi)
+
+        third = [gather(2, lo, hi) for lo, hi in HALVES]
+        shifted = [sb.tile([P, (hi - lo) * P], F32, name="shifted%d" % lo) for lo, hi in HALVES]
+        result = [sb.tile([P, (hi - lo) * P], F32, name="result%d" % lo) for lo, hi in HALVES]
+        for i, (lo, hi) in enumerate(HALVES):
+            nc.vector.tensor_tensor(shifted[i][:], third[i][:], s[:, columns(lo, hi)], ALU.add)
+        for i, ((lo, hi), queue) in enumerate(zip(HALVES, (nc.sync, nc.scalar))):
+            nc.vector.scalar_tensor_tensor(result[i][:], shifted[i][:], 0.0, totals[lo][:], ALU.max, ALU.add)
+            queue.dma_start(out=out[:, columns(lo, hi)], in_=result[i][:])

from contextlib import ExitStack

import concourse.mybir as mybir
from concourse.masks import make_identity

K, T, N = 512, 512, 128
FLOPS = 3 * 2 * K * T * N

F32 = mybir.dt.float32
BF16 = mybir.dt.bfloat16
I32 = mybir.dt.int32
U32 = mybir.dt.uint32
U16 = mybir.dt.uint16
U8 = mybir.dt.uint8
FP8X4 = mybir.dt.float8_e4m3fn_x4
ALU = mybir.AluOpType
ACT = mybir.ActivationFunctionType

P = 128
PACK = 4
QUADRANT = 32
LIST_COLS = P // 16

HALVES = ((0, 2), (2, 4))
SMALL_FIRST = ((0, 1), (1, 2), (2, 4))
SMALL_LAST = ((0, 2), (2, 3), (3, 4))


def columns(lo, hi):
    return slice(lo * P, hi * P)


def tile_picked_wfilmg_relu_l_kernel(tc, x_words, x_scales, w1, w2, w3, pos1, pos2, pos3, out):
    nc = tc.nc
    with ExitStack() as ctx:
        sb = ctx.enter_context(tc.tile_pool(name="sb", bufs=1))
        ps = ctx.enter_context(tc.psum_pool(name="ps", bufs=1))

        def bank(number, strips, name):
            return ps.tile([P, strips * P], F32, name=name, tag="bank%d" % number)

        x_plane = sb.tile([P, T], U8, name="x_plane", align_bytes=64)
        nc.gpsimd.memset(x_plane[:].bitcast(U32), 0)

        staged = {}

        def load_weight(name, w):
            staged[name] = sb.tile([P, PACK, N], F32, name="staged_" + name)
            nc.sync.dma_start(out=staged[name][:], in_=w.rearrange("(p t) m -> p t m", t=PACK))

        load_weight("w3", w3)
        load_weight("w1", w1)
        for q in range(P // QUADRANT):
            nc.sync.dma_start(
                out=x_plane[QUADRANT * q : QUADRANT * q + 4, :].bitcast(I32),
                in_=x_scales[0, 4 * q : 4 * q + 4, :].bitcast(I32),
            )
        x_codes = sb.tile([P, T], U32, name="x_codes", align_bytes=64)
        nc.sync.dma_start(out=x_codes[:].bitcast(I32), in_=x_words[0].rearrange("p n t -> p (n t)").bitcast(I32))
        load_weight("w2", w2)
        lists = [sb.tile([P, T // 16], U16, name="list%d" % d) for d in range(3)]
        for offsets, pos in zip(lists, (pos1, pos2, pos3)):
            nc.sync.dma_start(offsets[:], pos)

        identity = sb.tile([P, P], F32, name="identity")
        make_identity(nc, identity[:])

        grouped, codes, planes = {}, {}, {}
        for name in ("w3", "w1", "w2"):
            grouped[name] = sb.tile([P, N, PACK], BF16, name="grouped_" + name, tag="grouped_" + name, align_bytes=64)
            codes[name] = sb.tile([P, N], U32, name="codes_" + name, align_bytes=64)
            planes[name] = sb.tile([P, N], U8, name="plane_" + name, align_bytes=64)

        def quantise(name):
            nc.vector.tensor_copy(out=grouped[name][:], in_=staged[name][:].rearrange("p t m -> p m t"))
            nc.vector.quantize_mx(
                out=codes[name][:].bitcast(FP8X4),
                scales=planes[name][:],
                in_=grouped[name][:].rearrange("p m t -> p (m t)"),
            )

        def project(name, lo, hi, number):
            sums = bank(number, hi - lo, "%s_x%d" % (name, lo))
            nc.tensor.matmul_mx(
                out=sums[:],
                lhsT=codes[name][:].bitcast(FP8X4),
                lhsT_scale=planes[name][:],
                rhs=x_codes[:, columns(lo, hi)].bitcast(FP8X4),
                rhs_scale=x_plane[:, columns(lo, hi)],
                start=True,
                stop=True,
            )
            return sums

        quantise("w3")
        quantise("w1")
        h = sb.tile([P, T], F32, name="h")
        g = sb.tile([P, T], F32, name="g")
        s = sb.tile([P, T], F32, name="s")
        h_sums = [project("w3", lo, hi, i) for i, (lo, hi) in enumerate(HALVES)]
        g_sums = [project("w1", lo, hi, 2 + i) for i, (lo, hi) in enumerate(SMALL_FIRST)]
        for (lo, hi), sums in zip(HALVES, h_sums):
            nc.scalar.copy(out=h[:, columns(lo, hi)], in_=sums[:])
        quantise("w2")
        for (lo, hi), sums in zip(SMALL_FIRST, g_sums):
            nc.scalar.copy(out=g[:, columns(lo, hi)], in_=sums[:])
        for i, (lo, hi) in enumerate(SMALL_FIRST):
            nc.scalar.copy(out=s[:, columns(lo, hi)], in_=project("w2", lo, hi, 5 + i)[:])

        scaled = {}

        def gather(d, lo, hi, tag=None):
            name = "scaled%d_%d" % (d, lo)
            piece = sb.tile([P, (hi - lo) * P], F32, name=name, tag=tag or name, align_bytes=64)
            window = h[:].indirect(lists[d][:, lo * LIST_COLS : hi * LIST_COLS])
            nc.vector.tensor_tensor(piece[:], window, g[:, columns(lo, hi)], ALU.mult)
            for strip in range(lo, hi):
                scaled[d, strip] = piece[:, columns(strip - lo, strip - lo + 1)]
            return piece

        gather(0, *SMALL_FIRST[0])
        gather(0, *SMALL_FIRST[1], tag="grouped_w2")
        gather(0, *SMALL_FIRST[2])
        for lo, hi in SMALL_LAST:
            gather(1, lo, hi)

        film = {}
        for number, (d, lo, hi) in enumerate(((0, 0, 2), (0, 2, 4), (1, 0, 2), (1, 2, 3), (1, 3, 4))):
            film[d, lo] = bank(number, hi - lo, "film%d_%d" % (d, lo))
        totals = {lo: bank(5 + i, hi - lo, "total%d" % lo) for i, (lo, hi) in enumerate(HALVES)}
        rectified = [sb.tile([P, T], F32, name="rectified%d" % d) for d in range(2)]

        def turn(target, slot, source, start, stop):
            nc.tensor.matmul(
                target[:, columns(slot, slot + 1)], source, identity[:], start=start, stop=stop, is_transpose=True
            )

        def turn_s(d, lo, hi):
            for strip in range(lo, hi):
                turn(film[d, lo], strip - lo, s[:, columns(strip, strip + 1)], strip == lo, False)

        def rectify(d, lo, hi):
            nc.scalar.activation(rectified[d][:, columns(lo, hi)], film[d, lo][:], ACT.Relu)

        def turn_scaled(d, lo, hi):
            for strip in range(lo, hi):
                turn(film[d, lo], strip - lo, scaled[d, strip], False, strip == hi - 1)
            rectify(d, lo, hi)

        def turn_back(d, lo, hi):
            for strip in range(lo, hi):
                first, last = d == 0 and strip == lo, d == 1 and strip == hi - 1
                turn(totals[lo], strip - lo, rectified[d][:, columns(strip, strip + 1)], first, last)

        for strip in range(2):
            turn(film[0, 0], strip, scaled[0, strip], strip == 0, False)
            turn(film[0, 0], strip, s[:, columns(strip, strip + 1)], False, strip == 1)
        rectify(0, 0, 2)
        turn_s(1, 0, 2)
        turn_s(0, 2, 4)
        turn_scaled(0, 2, 4)
        turn_scaled(1, 0, 2)
        turn_back(0, 0, 2)
        for lo, hi in SMALL_LAST[1:]:
            turn_s(1, lo, hi)
            turn_scaled(1, lo, hi)
        turn_back(0, 2, 4)
        for lo, hi in HALVES:
            turn_back(1, lo, hi)

        third = [gather(2, lo, hi) for lo, hi in HALVES]
        shifted = [sb.tile([P, (hi - lo) * P], F32, name="shifted%d" % lo) for lo, hi in HALVES]
        result = [sb.tile([P, (hi - lo) * P], F32, name="result%d" % lo) for lo, hi in HALVES]
        for i, (lo, hi) in enumerate(HALVES):
            nc.vector.tensor_tensor(shifted[i][:], third[i][:], s[:, columns(lo, hi)], ALU.add)
        for i, ((lo, hi), queue) in enumerate(zip(HALVES, (nc.sync, nc.scalar))):
            nc.vector.scalar_tensor_tensor(result[i][:], shifted[i][:], 0.0, totals[lo][:], ALU.max, ALU.add)
            queue.dma_start(out=out[:, columns(lo, hi)], in_=result[i][:])
